import numpy as np
import ml_dtypes


def mxq(x, axis, fmt="e4m3"):
    dtype, down = {"e4m3": (ml_dtypes.float8_e4m3fn, 7), "e5m2": (ml_dtypes.float8_e5m2, 14)}[fmt]
    v = np.moveaxis(np.asarray(x, np.float32).astype(ml_dtypes.bfloat16).astype(np.float64), axis, -1)
    blocks = v.reshape(v.shape[:-1] + (-1, 32))
    amax = np.abs(blocks).max(-1, keepdims=True)
    byte = np.maximum(np.where(amax > 0, np.frexp(amax)[1] - 1 + 127, 0) - down, 1)
    scale = np.exp2(byte - 127.0)
    codes = (blocks / scale).astype(np.float32).astype(dtype).astype(np.float64)
    return np.moveaxis((codes * scale).reshape(v.shape), -1, axis)


WIDE = False


def mx_kscale(k):
    if not WIDE:
        return np.ones(k)
    levels = np.array([10, -10, 5, -5, 0])
    if k % 512:
        return np.exp2(np.random.permutation(np.resize(levels, k // 32))).repeat(32)
    a = np.empty((k // 512, 16))
    for p in range(k // 512):
        a[p, :8] = np.random.permutation(np.resize(levels, 8))
        for g in range(8):
            far = levels[np.abs(levels - a[p, g]) >= 10]
            a[p, g + 8] = far[np.random.randint(len(far))]
    return np.exp2(a.ravel()).repeat(32)


def f64(x):
    return np.asarray(x).astype(np.float64)


def striped(idx):
    return np.tile(np.asarray(idx).reshape(-1, 16).T, (8, 1)).astype(np.uint16)


def unstriped(offs):
    return offs[:16].T.reshape(-1).astype(np.int64)


E2M1 = np.array([0.0, 0.5, 1.0, 1.5, 2.0, 3.0, 4.0, 6.0, -0.0, -0.5, -1.0, -1.5, -2.0, -3.0, -4.0, -6.0])


def pack_weight(w, fmt):
    k, n = w.shape
    w = f64(np.asarray(w, np.float32).astype(ml_dtypes.bfloat16)).reshape(k // 32, 32, n)
    amax = np.abs(w).max(1)
    if fmt == "e4m3":
        byte = np.frexp(amax)[1] - 1 + 127 - 7
    else:
        mant, ex = np.frexp(amax / 6.0)
        byte = np.where(mant > 0.5, ex, ex - 1) + 127
    byte = np.clip(np.where(amax > 0, byte, 1), 1, 254)
    scaled = (w * np.exp2(127.0 - byte)[:, None, :]).reshape(k, n).astype(np.float32)
    by_word = np.ascontiguousarray(scaled.reshape(k // 512, 128, 4, n).transpose(0, 1, 3, 2))
    if fmt == "e4m3":
        words = by_word.astype(ml_dtypes.float8_e4m3fn).view(np.uint8)
    else:
        c = by_word.astype(ml_dtypes.float4_e2m1fn).view(np.uint8) & 0xF
        words = (c[..., 0::2] | (c[..., 1::2] << 4)).reshape(k // 512, 128, 2 * n)
    return np.ascontiguousarray(words), np.ascontiguousarray(byte.astype(np.uint8).reshape(k // 512, 16, n))


def unpack_weight(words, scales, fmt):
    g, _, n = scales.shape
    words = np.ascontiguousarray(words).reshape(g, 128, n, -1)
    if fmt == "e4m3":
        vals = words.view(ml_dtypes.float8_e4m3fn).astype(np.float64)
    else:
        nib = np.empty((g, 128, n, 4), np.uint8)
        nib[..., 0::2] = words & 0xF
        nib[..., 1::2] = words >> 4
        vals = E2M1[nib]
    vals = vals * np.repeat(np.exp2(scales.astype(np.float64) - 127.0), 8, axis=1)[..., None]
    return vals.transpose(0, 1, 3, 2).reshape(g * 512, n)


D, T, I, Q = 512, 1024, 512, 256


def setup_inputs():
    n = np.random.standard_normal
    idx = np.random.permutation(T)[:I]
    fi = mx_kscale(I)
    fd = mx_kscale(D)
    ti = np.ones(T)
    ti[idx] = fi
    atomp = pack_weight(n((D, T)) / fd[:, None], "e4m3")
    return {
        "rows": (n((D, T)) * 0.5 / np.sqrt(D) / ti).astype(np.float32),
        "code0": (np.maximum(n((I, Q)), 0.0)).astype(np.float32),
        "cs1": (np.random.uniform(0.5, 2.0, (I, 1)) * fi[:, None]).astype(np.float32),
        "sig": (n((D, Q)) * 2.0).astype(np.float32),
        "fsc": (np.random.uniform(0.03, 0.06, (D, 1)) * fd[:, None]).astype(np.float32),
        "atom_words": atomp[0],
        "atom_scales": atomp[1],
        "rate": (np.random.uniform(0.3, 1.0, (I, 1))).astype(np.float32),
        "th": (np.random.uniform(0.0, 0.5, (I, 1))).astype(np.float32),
        "offs": striped(idx),
    }


def reference(rows, code0, cs1, sig, fsc, atom_words, atom_scales, rate, th, offs):
    idx = unstriped(offs)
    atomu = unpack_weight(atom_words, atom_scales, "e4m3")
    rt = f64(rows)[:, idx].T
    cw1 = f64(code0) * f64(cs1)
    rtq = mxq(rt, 0, "e4m3")
    cw1q = mxq(cw1, 0, "e4m3")
    r = rtq.T @ cw1q
    e = (f64(sig) - r) * f64(fsc)
    atomidxg = atomu[:, idx]
    eq = mxq(e, 0, "e4m3")
    a = atomidxg.T @ eq
    y = np.maximum(f64(code0) + a * f64(rate) - f64(th), 0.0)
    return y

@@ -1,0 +1,179 @@
+from contextlib import ExitStack
+
+import concourse.mybir as mybir
+from concourse.masks import make_identity
+
+D, T, I, Q = 512, 1024, 512, 256
+FLOPS = 2 * 2 * D * I * Q
+
+F32 = mybir.dt.float32
+BF16 = mybir.dt.bfloat16
+I32 = mybir.dt.int32
+U32 = mybir.dt.uint32
+U16 = mybir.dt.uint16
+U8 = mybir.dt.uint8
+FP8X4 = mybir.dt.float8_e4m3fn_x4
+ALU = mybir.AluOpType
+ACT = mybir.ActivationFunctionType
+
+P = 128
+PACK = 4
+HALF = Q // 2
+
+
+def walk_planes(ap):
+    return ap.rearrange("p t (c i) -> p c t i", i=4)
+
+
+def walk_grouped(ap):
+    return ap.rearrange("p (c i) t -> p c t i", i=4)
+
+
+def tile_attend_pursuitstep_kernel(tc, rows, code0, cs1, sig, fsc, atom_words, atom_scales, rate, th, offs, out):
+    nc = tc.nc
+    with ExitStack() as ctx:
+        sb = ctx.enter_context(tc.tile_pool(name="sb", bufs=1))
+        ps = ctx.enter_context(tc.psum_pool(name="ps", bufs=1))
+
+        offsets = sb.tile([P, I // 16], U16, name="offsets")
+        nc.sync.dma_start(offsets[:], offs)
+
+        rows_k = rows.rearrange("(p t) c -> t p c", t=PACK)
+
+        def load_plane(j):
+            plane = sb.tile([P, T], F32, name=f"plane{j}", tag=f"plane{j}", align_bytes=64)
+            nc.sync.dma_start(plane[:], rows_k[j])
+            return plane
+
+        planes = [load_plane(0), load_plane(1)]
+        cs_k = sb.tile([P, PACK], F32, name="cs_k")
+        nc.sync.dma_start(cs_k[:], cs1.rearrange("(p t) o -> p (t o)", t=PACK))
+        atom_sc = sb.tile([P, T], U8, name="atom_sc", tag="atom_sc", align_bytes=64)
+        nc.vector.memset(atom_sc[:].bitcast(I32), 0)
+        for r in range(4):
+            nc.sync.dma_start(atom_sc[r:P:32, :].bitcast(I32), atom_scales[0, r:16:4, :].bitcast(I32))
+        planes.extend([load_plane(2), load_plane(3)])
+        code_k = sb.tile([P, PACK, Q], F32, name="code_k", tag="code_k", align_bytes=64)
+        nc.sync.dma_start(code_k[:], code0.rearrange("(p t) q -> p t q", t=PACK))
+        fsc_k = sb.tile([P, PACK], F32, name="fsc_k")
+        nc.sync.dma_start(fsc_k[:], fsc.rearrange("(p t) o -> p (t o)", t=PACK))
+        sig_k = sb.tile([P, PACK, Q], F32, name="sig_k")
+        nc.sync.dma_start(sig_k[:], sig.rearrange("(p t) q -> p t q", t=PACK))
+        atom_w = sb.tile([P, T], I32, name="atom_w", align_bytes=64)
+        nc.sync.dma_start(atom_w[:], atom_words[0].rearrange("p n t -> p (n t)").bitcast(I32))
+        rate_m = sb.tile([P, PACK], F32, name="rate_m")
+        th_m = sb.tile([P, PACK], F32, name="th_m")
+        with nc.allow_non_contiguous_dma(reason="one value a partition and tile"):
+            nc.sync.dma_start(rate_m[:], rate.rearrange("(j m) o -> m (j o)", m=P))
+            nc.sync.dma_start(th_m[:], th.rearrange("(j m) o -> m (j o)", m=P))
+        code_m = sb.tile([P, PACK, Q], F32, name="code_m")
+        nc.sync.dma_start(code_m[:], code0.rearrange("(j m) q -> m j q", m=P))
+
+        ident = sb.tile([P, P], F32, name="ident")
+        make_identity(nc, ident[:])
+
+        def turn(j, g, rt):
+            words = g[:].bitcast(F32)
+            xt = ps.tile([P, 2, P], F32, name=f"xt{j}", tag=f"bank{j}")
+            for u in range(2):
+                nc.tensor.transpose(xt[:, u, :], words[:, u : I // 2 : 2], ident[:])
+            nc.scalar.copy(rt.bitcast(F32), xt[:].rearrange("s u p -> s p u"))
+
+        def quantise(name, rt, width, tag):
+            w = sb.tile([P, width], U32, name=f"rt_w{name}", tag=tag, align_bytes=64)
+            s = sb.tile([P, width], U8, name=f"rt_s{name}", align_bytes=64)
+            nc.vector.quantize_mx(out=w[:].bitcast(FP8X4), scales=s[:], in_=rt)
+            return w, s
+
+        def gather(j, tag):
+            g = sb.tile([P, I], BF16, name=f"g{j}", tag=tag, align_bytes=64)
+            nc.vector.tensor_copy(g[:], planes[j][:].indirect(offsets[:]))
+            return g
+
+        g0 = gather(0, "g0")
+        plane1_bf = sb.tile([P, T], BF16, name="plane1_bf", tag="rt0", align_bytes=64)
+        nc.scalar.activation(plane1_bf[:], planes[1][:], ACT.Copy)
+        g1 = sb.tile([P, I], BF16, name="g1", align_bytes=64)
+        nc.scalar.activation(g1[:], plane1_bf[:].indirect(offsets[:]), ACT.Copy)
+        atom_sc_g = [sb.tile([P, I // 2], U8, name="atom_sc_g0", align_bytes=64)]
+        nc.vector.tensor_copy(atom_sc_g[0][:], atom_sc[:].indirect(offsets[:, :16]))
+        g2 = gather(2, "g2")
+        g3 = gather(3, "g3")
+        rt0 = sb.tile([P, P, PACK], BF16, name="rt0", tag="rt0", align_bytes=64)
+        rt12 = sb.tile([P, 2 * P, PACK], BF16, name="rt12", align_bytes=64)
+        rt3 = sb.tile([P, P, PACK], BF16, name="rt3", tag="rt3", align_bytes=64)
+        turn(0, g0, rt0[:])
+        turn(1, g1, rt12[:, :P, :])
+        turn(2, g2, rt12[:, P:, :])
+        turn(3, g3, rt3[:])
+
+        w0, s0 = quantise("0", rt0[:].rearrange("s p t -> s (p t)"), P, "plane3")
+        cw = sb.tile([P, Q, PACK], BF16, name="cw", tag="cw", align_bytes=64)
+        nc.vector.tensor_tensor(
+            walk_grouped(cw[:]),
+            walk_planes(code_k[:]),
+            cs_k[:].unsqueeze(1).unsqueeze(3).to_broadcast([P, Q // 4, PACK, 4]),
+            ALU.mult,
+        )
+        cw_w = sb.tile([P, Q], U32, name="cw_w", align_bytes=64)
+        cw_s = sb.tile([P, Q], U8, name="cw_s", align_bytes=64)
+        nc.vector.quantize_mx(out=cw_w[:].bitcast(FP8X4), scales=cw_s[:], in_=cw[:].rearrange("p q t -> p (q t)"))
+        w12, s12 = quantise("12", rt12[:].rearrange("s p t -> s (p t)"), 2 * P, "cw")
+        w3, s3 = quantise("3", rt3[:].rearrange("s p t -> s (p t)"), P, "rt_w3")
+        rtq = [(w0[:], s0[:]), (w12[:, :P], s12[:, :P]), (w12[:, P:], s12[:, P:]), (w3[:], s3[:])]
+
+        sf = sb.tile([P, PACK, Q], F32, name="sf")
+        for j in range(PACK):
+            nc.scalar.activation(sf[:, j, :], sig_k[:, j, :], ACT.Copy, scale=fsc_k[:, j : j + 1])
+        neg_fsc = sb.tile([P, PACK], F32, name="neg_fsc")
+        nc.scalar.activation(neg_fsc[:], fsc_k[:], ACT.Copy, scale=-1.0)
+        neg_th = sb.tile([P, PACK], F32, name="neg_th")
+        nc.scalar.activation(neg_th[:], th_m[:], ACT.Copy, scale=-1.0)
+
+        atom_w_g = [sb.tile([P, I // 2], U32, name="atom_w_g0", tag="rt3", align_bytes=64)]
+        nc.vector.tensor_copy(atom_w_g[0][:], atom_w[:].bitcast(U32).indirect(offsets[:, :16]))
+
+        e_planes = sb.tile([P, PACK, Q], BF16, name="e_planes", align_bytes=64)
+        for j in range(PACK):
+            w, s = rtq[j]
+            r = ps.tile([P, Q], F32, name=f"r{j}", tag=f"bank{4 + j}")
+            nc.tensor.matmul_mx(
+                out=r[:], lhsT=w.bitcast(FP8X4), lhsT_scale=s,
+                rhs=cw_w[:].bitcast(FP8X4), rhs_scale=cw_s[:], start=True, stop=True,
+            )
+            nc.vector.scalar_tensor_tensor(
+                e_planes[:, j, :], r[:], neg_fsc[:, j : j + 1], sf[:, j, :], ALU.mult, ALU.add
+            )
+
+        e_w = sb.tile([P, Q], U32, name="e_w", align_bytes=64)
+        e_s = sb.tile([P, Q], U8, name="e_s", align_bytes=64)
+        es = []
+        for h in range(2):
+            cols = slice(h * HALF, (h + 1) * HALF)
+            e = sb.tile([P, HALF, PACK], BF16, name=f"e{h}", tag=f"e{h}", align_bytes=64)
+            nc.vector.tensor_copy(walk_grouped(e[:]), walk_planes(e_planes[:, :, cols]))
+            es.append(e)
+        for h in range(2):
+            cols = slice(h * HALF, (h + 1) * HALF)
+            nc.vector.quantize_mx(
+                out=e_w[:, cols].bitcast(FP8X4), scales=e_s[:, cols], in_=es[h][:].rearrange("p q t -> p (q t)")
+            )
+
+        atom_sc_g.append(sb.tile([P, I // 2], U8, name="atom_sc_g1", tag="e0", align_bytes=64))
+        nc.vector.tensor_copy(atom_sc_g[1][:], atom_sc[:].indirect(offsets[:, 16:]))
+        atom_w_g.append(sb.tile([P, I // 2], U32, name="atom_w_g1", tag="e1", align_bytes=64))
+        nc.vector.tensor_copy(atom_w_g[1][:], atom_w[:].bitcast(U32).indirect(offsets[:, 16:]))
+
+        for j in range(PACK):
+            cols = slice(j * P, (j + 1) * P)
+            a = ps.tile([P, Q], F32, name=f"a{j}", tag=f"bank{j}")
+            nc.tensor.matmul_mx(
+                out=a[:], lhsT=atom_w_g[j // 2][:, (j % 2) * P : (j % 2 + 1) * P].bitcast(FP8X4),
+                lhsT_scale=atom_sc_g[j // 2][:, (j % 2) * P : (j % 2 + 1) * P],
+                rhs=e_w[:].bitcast(FP8X4), rhs_scale=e_s[:], start=True, stop=True,
+            )
+            x = sb.tile([P, Q], F32, name=f"x{j}")
+            nc.vector.scalar_tensor_tensor(x[:], a[:], rate_m[:, j : j + 1], code_m[:, j, :], ALU.mult, ALU.add)
+            y = sb.tile([P, Q], F32, name=f"y{j}")
+            nc.scalar.activation(y[:], x[:], ACT.Relu, bias=neg_th[:, j : j + 1])
+            nc.sync.dma_start(out[cols, :], y[:])

@@ -33,34 +33,32 @@ def tile_attend_pursuitstep_kernel(tc, rows, code0, cs1, sig, fsc, atom_words, a
     nc = tc.nc
     with ExitStack() as ctx:
         sb = ctx.enter_context(tc.tile_pool(name="sb", bufs=1))
+        last = ctx.enter_context(tc.tile_pool(name="last", bufs=1))
         ps = ctx.enter_context(tc.psum_pool(name="ps", bufs=1))
 
         offsets = sb.tile([P, I // 16], U16, name="offsets")
         nc.sync.dma_start(offsets[:], offs)
-
-        rows_k = rows.rearrange("(p t) c -> t p c", t=PACK)
-
-        def load_plane(j):
-            plane = sb.tile([P, T], F32, name=f"plane{j}", tag=f"plane{j}", align_bytes=64)
-            nc.sync.dma_start(plane[:], rows_k[j])
-            return plane
-
-        planes = [load_plane(0), load_plane(1)]
         cs_k = sb.tile([P, PACK], F32, name="cs_k")
         nc.sync.dma_start(cs_k[:], cs1.rearrange("(p t) o -> p (t o)", t=PACK))
-        atom_sc = sb.tile([P, T], U8, name="atom_sc", tag="atom_sc", align_bytes=64)
+        code_k = sb.tile([P, PACK, Q], F32, name="code_k")
+        nc.sync.dma_start(code_k[:], code0.rearrange("(p t) q -> p t q", t=PACK))
+
+        rows_k = rows.rearrange("(p t) c -> t p c", t=PACK)
+        planes = [sb.tile([P, T], F32, name=f"plane{j}", align_bytes=64) for j in range(PACK - 1)]
+        planes.append(last.tile([P, T], F32, name="plane3", align_bytes=64, offset=0))
+        nc.sync.dma_start(planes[0][:], rows_k[0])
+        atom_sc = sb.tile([P, T], U8, name="atom_sc", align_bytes=64)
         nc.vector.memset(atom_sc[:].bitcast(I32), 0)
         for r in range(4):
             nc.sync.dma_start(atom_sc[r:P:32, :].bitcast(I32), atom_scales[0, r:16:4, :].bitcast(I32))
-        planes.extend([load_plane(2), load_plane(3)])
-        code_k = sb.tile([P, PACK, Q], F32, name="code_k", tag="code_k", align_bytes=64)
-        nc.sync.dma_start(code_k[:], code0.rearrange("(p t) q -> p t q", t=PACK))
+        for j in range(1, PACK):
+            nc.sync.dma_start(planes[j][:], rows_k[j])
+        atom_w = sb.tile([P, T], I32, name="atom_w", align_bytes=64)
+        nc.sync.dma_start(atom_w[:], atom_words[0].rearrange("p n t -> p (n t)").bitcast(I32))
         fsc_k = sb.tile([P, PACK], F32, name="fsc_k")
         nc.sync.dma_start(fsc_k[:], fsc.rearrange("(p t) o -> p (t o)", t=PACK))
         sig_k = sb.tile([P, PACK, Q], F32, name="sig_k")
         nc.sync.dma_start(sig_k[:], sig.rearrange("(p t) q -> p t q", t=PACK))
-        atom_w = sb.tile([P, T], I32, name="atom_w", align_bytes=64)
-        nc.sync.dma_start(atom_w[:], atom_words[0].rearrange("p n t -> p (n t)").bitcast(I32))
         rate_m = sb.tile([P, PACK], F32, name="rate_m")
         th_m = sb.tile([P, PACK], F32, name="th_m")
         with nc.allow_non_contiguous_dma(reason="one value a partition and tile"):
@@ -72,43 +70,7 @@ def tile_attend_pursuitstep_kernel(tc, rows, code0, cs1, sig, fsc, atom_words, a
         ident = sb.tile([P, P], F32, name="ident")
         make_identity(nc, ident[:])
 
-        def turn(j, g, rt):
-            words = g[:].bitcast(F32)
-            xt = ps.tile([P, 2, P], F32, name=f"xt{j}", tag=f"bank{j}")
-            for u in range(2):
-                nc.tensor.transpose(xt[:, u, :], words[:, u : I // 2 : 2], ident[:])
-            nc.scalar.copy(rt.bitcast(F32), xt[:].rearrange("s u p -> s p u"))
-
-        def quantise(name, rt, width, tag):
-            w = sb.tile([P, width], U32, name=f"rt_w{name}", tag=tag, align_bytes=64)
-            s = sb.tile([P, width], U8, name=f"rt_s{name}", align_bytes=64)
-            nc.vector.quantize_mx(out=w[:].bitcast(FP8X4), scales=s[:], in_=rt)
-            return w, s
-
-        def gather(j, tag):
-            g = sb.tile([P, I], BF16, name=f"g{j}", tag=tag, align_bytes=64)
-            nc.vector.tensor_copy(g[:], planes[j][:].indirect(offsets[:]))
-            return g
-
-        g0 = gather(0, "g0")
-        plane1_bf = sb.tile([P, T], BF16, name="plane1_bf", tag="rt0", align_bytes=64)
-        nc.scalar.activation(plane1_bf[:], planes[1][:], ACT.Copy)
-        g1 = sb.tile([P, I], BF16, name="g1", align_bytes=64)
-        nc.scalar.activation(g1[:], plane1_bf[:].indirect(offsets[:]), ACT.Copy)
-        atom_sc_g = [sb.tile([P, I // 2], U8, name="atom_sc_g0", align_bytes=64)]
-        nc.vector.tensor_copy(atom_sc_g[0][:], atom_sc[:].indirect(offsets[:, :16]))
-        g2 = gather(2, "g2")
-        g3 = gather(3, "g3")
-        rt0 = sb.tile([P, P, PACK], BF16, name="rt0", tag="rt0", align_bytes=64)
-        rt12 = sb.tile([P, 2 * P, PACK], BF16, name="rt12", align_bytes=64)
-        rt3 = sb.tile([P, P, PACK], BF16, name="rt3", tag="rt3", align_bytes=64)
-        turn(0, g0, rt0[:])
-        turn(1, g1, rt12[:, :P, :])
-        turn(2, g2, rt12[:, P:, :])
-        turn(3, g3, rt3[:])
-
-        w0, s0 = quantise("0", rt0[:].rearrange("s p t -> s (p t)"), P, "plane3")
-        cw = sb.tile([P, Q, PACK], BF16, name="cw", tag="cw", align_bytes=64)
+        cw = sb.tile([P, Q, PACK], BF16, name="cw", align_bytes=64)
         nc.vector.tensor_tensor(
             walk_grouped(cw[:]),
             walk_planes(code_k[:]),
@@ -118,20 +80,54 @@ def tile_attend_pursuitstep_kernel(tc, rows, code0, cs1, sig, fsc, atom_words, a
         cw_w = sb.tile([P, Q], U32, name="cw_w", align_bytes=64)
         cw_s = sb.tile([P, Q], U8, name="cw_s", align_bytes=64)
         nc.vector.quantize_mx(out=cw_w[:].bitcast(FP8X4), scales=cw_s[:], in_=cw[:].rearrange("p q t -> p (q t)"))
-        w12, s12 = quantise("12", rt12[:].rearrange("s p t -> s (p t)"), 2 * P, "cw")
-        w3, s3 = quantise("3", rt3[:].rearrange("s p t -> s (p t)"), P, "rt_w3")
-        rtq = [(w0[:], s0[:]), (w12[:, :P], s12[:, :P]), (w12[:, P:], s12[:, P:]), (w3[:], s3[:])]
+        atom_sc_g = [sb.tile([P, I // 2], U8, name="atom_sc_g0", align_bytes=64)]
+        nc.vector.tensor_copy(atom_sc_g[0][:], atom_sc[:].indirect(offsets[:, :16]))
 
+        def turn(j, g, rt):
+            words = g[:].bitcast(F32)
+            xt = ps.tile([P, 2, P], F32, name=f"xt{j}", tag=f"bank{j}")
+            for u in range(2):
+                nc.tensor.transpose(xt[:, u, :], words[:, u : I // 2 : 2], ident[:])
+            nc.scalar.copy(rt.bitcast(F32), xt[:].rearrange("s u p -> s p u"))
+
+        plane0_bf = sb.tile([P, T], BF16, name="plane0_bf", align_bytes=64)
+        nc.scalar.activation(plane0_bf[:], planes[0][:], ACT.Copy)
+        gs = [sb.tile([P, I], BF16, name=f"g{j}", align_bytes=64) for j in range(PACK)]
+        nc.scalar.activation(gs[0][:], plane0_bf[:].indirect(offsets[:]), ACT.Copy)
+        for j in range(1, PACK):
+            nc.vector.tensor_copy(gs[j][:], planes[j][:].indirect(offsets[:]))
+        rt01 = sb.tile([P, 2 * P, PACK], BF16, name="rt01", align_bytes=64)
+        rt2 = sb.tile([P, P, PACK], BF16, name="rt2", align_bytes=64)
+        rt3 = sb.tile([P, P, PACK], BF16, name="rt3", align_bytes=64)
+        turn(0, gs[0], rt01[:, :P, :])
+        turn(1, gs[1], rt01[:, P:, :])
+        turn(2, gs[2], rt2[:])
+        turn(3, gs[3], rt3[:])
+
+        def quantise(w, name, rt):
+            s = sb.tile([P, w.shape[1]], U8, name=f"rt_s{name}", align_bytes=64)
+            nc.vector.quantize_mx(out=w[:].bitcast(FP8X4), scales=s[:], in_=rt[:].rearrange("s p t -> s (p t)"))
+            return s
+
+        w01 = last.tile([P, 2 * P], U32, name="rt_w01", align_bytes=64, offset=0)
+        s01 = quantise(w01, "01", rt01)
+        atom_sc_g.append(last.tile([P, I // 2], U8, name="atom_sc_g1", align_bytes=64, offset=1024))
+        nc.vector.tensor_copy(atom_sc_g[1][:], atom_sc[:].indirect(offsets[:, 16:]))
+        w2 = sb.tile([P, P], U32, name="rt_w2", align_bytes=64)
+        s2 = quantise(w2, "2", rt2)
+        atom_w_g = [sb.tile([P, I // 2], U32, name="atom_w_g0", align_bytes=64)]
+        nc.vector.tensor_copy(atom_w_g[0][:], atom_w[:].bitcast(U32).indirect(offsets[:, :16]))
+        w3 = sb.tile([P, P], U32, name="rt_w3", align_bytes=64)
+        s3 = quantise(w3, "3", rt3)
+        rtq = [(w01[:, :P], s01[:, :P]), (w01[:, P:], s01[:, P:]), (w2[:], s2[:]), (w3[:], s3[:])]
+
+        neg_fsc = sb.tile([P, PACK], F32, name="neg_fsc")
+        nc.gpsimd.tensor_scalar(neg_fsc[:], fsc_k[:], -1.0, 0.0, ALU.mult, ALU.add)
         sf = sb.tile([P, PACK, Q], F32, name="sf")
         for j in range(PACK):
             nc.scalar.activation(sf[:, j, :], sig_k[:, j, :], ACT.Copy, scale=fsc_k[:, j : j + 1])
-        neg_fsc = sb.tile([P, PACK], F32, name="neg_fsc")
-        nc.scalar.activation(neg_fsc[:], fsc_k[:], ACT.Copy, scale=-1.0)
         neg_th = sb.tile([P, PACK], F32, name="neg_th")
-        nc.scalar.activation(neg_th[:], th_m[:], ACT.Copy, scale=-1.0)
-
-        atom_w_g = [sb.tile([P, I // 2], U32, name="atom_w_g0", tag="rt3", align_bytes=64)]
-        nc.vector.tensor_copy(atom_w_g[0][:], atom_w[:].bitcast(U32).indirect(offsets[:, :16]))
+        nc.gpsimd.tensor_scalar(neg_th[:], th_m[:], -1.0, 0.0, ALU.mult, ALU.add)
 
         e_planes = sb.tile([P, PACK, Q], BF16, name="e_planes", align_bytes=64)
         for j in range(PACK):
@@ -147,33 +143,31 @@ def tile_attend_pursuitstep_kernel(tc, rows, code0, cs1, sig, fsc, atom_words, a
 
         e_w = sb.tile([P, Q], U32, name="e_w", align_bytes=64)
         e_s = sb.tile([P, Q], U8, name="e_s", align_bytes=64)
-        es = []
-        for h in range(2):
-            cols = slice(h * HALF, (h + 1) * HALF)
-            e = sb.tile([P, HALF, PACK], BF16, name=f"e{h}", tag=f"e{h}", align_bytes=64)
-            nc.vector.tensor_copy(walk_grouped(e[:]), walk_planes(e_planes[:, :, cols]))
-            es.append(e)
+        es = [sb.tile([P, HALF, PACK], BF16, name=f"e{h}", tag=f"e{h}", align_bytes=64) for h in range(2)]
+        nc.vector.tensor_copy(walk_grouped(es[0][:]), walk_planes(e_planes[:, :, :HALF]))
+        nc.scalar.copy(walk_grouped(es[1][:]), walk_planes(e_planes[:, :, HALF:]))
         for h in range(2):
             cols = slice(h * HALF, (h + 1) * HALF)
             nc.vector.quantize_mx(
                 out=e_w[:, cols].bitcast(FP8X4), scales=e_s[:, cols], in_=es[h][:].rearrange("p q t -> p (q t)")
             )
 
-        atom_sc_g.append(sb.tile([P, I // 2], U8, name="atom_sc_g1", tag="e0", align_bytes=64))
-        nc.vector.tensor_copy(atom_sc_g[1][:], atom_sc[:].indirect(offsets[:, 16:]))
         atom_w_g.append(sb.tile([P, I // 2], U32, name="atom_w_g1", tag="e1", align_bytes=64))
         nc.vector.tensor_copy(atom_w_g[1][:], atom_w[:].bitcast(U32).indirect(offsets[:, 16:]))
 
         for j in range(PACK):
             cols = slice(j * P, (j + 1) * P)
+            part = slice((j % 2) * P, (j % 2 + 1) * P)
             a = ps.tile([P, Q], F32, name=f"a{j}", tag=f"bank{j}")
             nc.tensor.matmul_mx(
-                out=a[:], lhsT=atom_w_g[j // 2][:, (j % 2) * P : (j % 2 + 1) * P].bitcast(FP8X4),
-                lhsT_scale=atom_sc_g[j // 2][:, (j % 2) * P : (j % 2 + 1) * P],
+                out=a[:], lhsT=atom_w_g[j // 2][:, part].bitcast(FP8X4), lhsT_scale=atom_sc_g[j // 2][:, part],
                 rhs=e_w[:].bitcast(FP8X4), rhs_scale=e_s[:], start=True, stop=True,
             )
             x = sb.tile([P, Q], F32, name=f"x{j}")
             nc.vector.scalar_tensor_tensor(x[:], a[:], rate_m[:, j : j + 1], code_m[:, j, :], ALU.mult, ALU.add)
             y = sb.tile([P, Q], F32, name=f"y{j}")
-            nc.scalar.activation(y[:], x[:], ACT.Relu, bias=neg_th[:, j : j + 1])
+            if j < PACK - 1:
+                nc.scalar.activation(y[:], x[:], ACT.Relu, bias=neg_th[:, j : j + 1])
+            else:
+                nc.vector.tensor_scalar(y[:], x[:], th_m[:, j : j + 1], 0.0, ALU.subtract, ALU.max)
             nc.sync.dma_start(out[cols, :], y[:])

@@ -59,11 +59,10 @@ def tile_attend_pursuitstep_kernel(tc, rows, code0, cs1, sig, fsc, atom_words, a
         nc.sync.dma_start(fsc_k[:], fsc.rearrange("(p t) o -> p (t o)", t=PACK))
         sig_k = sb.tile([P, PACK, Q], F32, name="sig_k")
         nc.sync.dma_start(sig_k[:], sig.rearrange("(p t) q -> p t q", t=PACK))
-        rate_m = sb.tile([P, PACK], F32, name="rate_m")
-        th_m = sb.tile([P, PACK], F32, name="th_m")
-        with nc.allow_non_contiguous_dma(reason="one value a partition and tile"):
-            nc.sync.dma_start(rate_m[:], rate.rearrange("(j m) o -> m (j o)", m=P))
-            nc.sync.dma_start(th_m[:], th.rearrange("(j m) o -> m (j o)", m=P))
+        vec_rows = sb.tile([P, P], F32, name="vec_rows")
+        nc.gpsimd.memset(vec_rows[:], 0.0)
+        nc.sync.dma_start(vec_rows[0:PACK, :], rate.rearrange("(j m) o -> j (m o)", m=P))
+        nc.sync.dma_start(vec_rows[PACK : 2 * PACK, :], th.rearrange("(j m) o -> j (m o)", m=P))
         code_m = sb.tile([P, PACK, Q], F32, name="code_m")
         nc.sync.dma_start(code_m[:], code0.rearrange("(j m) q -> m j q", m=P))
 
@@ -80,8 +79,8 @@ def tile_attend_pursuitstep_kernel(tc, rows, code0, cs1, sig, fsc, atom_words, a
         cw_w = sb.tile([P, Q], U32, name="cw_w", align_bytes=64)
         cw_s = sb.tile([P, Q], U8, name="cw_s", align_bytes=64)
         nc.vector.quantize_mx(out=cw_w[:].bitcast(FP8X4), scales=cw_s[:], in_=cw[:].rearrange("p q t -> p (q t)"))
-        atom_sc_g = [sb.tile([P, I // 2], U8, name="atom_sc_g0", align_bytes=64)]
-        nc.vector.tensor_copy(atom_sc_g[0][:], atom_sc[:].indirect(offsets[:, :16]))
+        sc_early = sb.tile([P, 3 * P], U8, name="sc_early", align_bytes=64)
+        nc.vector.tensor_copy(sc_early[:], atom_sc[:].indirect(offsets[:, :24]))
 
         def turn(j, g, rt):
             words = g[:].bitcast(F32)
@@ -111,8 +110,9 @@ def tile_attend_pursuitstep_kernel(tc, rows, code0, cs1, sig, fsc, atom_words, a
 
         w01 = last.tile([P, 2 * P], U32, name="rt_w01", align_bytes=64, offset=0)
         s01 = quantise(w01, "01", rt01)
-        atom_sc_g.append(last.tile([P, I // 2], U8, name="atom_sc_g1", align_bytes=64, offset=1024))
-        nc.vector.tensor_copy(atom_sc_g[1][:], atom_sc[:].indirect(offsets[:, 16:]))
+        sc_late = last.tile([P, P], U8, name="sc_late", align_bytes=64, offset=1024)
+        nc.vector.tensor_copy(sc_late[:], atom_sc[:].indirect(offsets[:, 24:]))
+        atom_sc_g = [sc_early[:, j * P : (j + 1) * P] for j in range(PACK - 1)] + [sc_late[:]]
         w2 = sb.tile([P, P], U32, name="rt_w2", align_bytes=64)
         s2 = quantise(w2, "2", rt2)
         atom_w_g = [sb.tile([P, I // 2], U32, name="atom_w_g0", align_bytes=64)]
@@ -126,8 +126,12 @@ def tile_attend_pursuitstep_kernel(tc, rows, code0, cs1, sig, fsc, atom_words, a
         sf = sb.tile([P, PACK, Q], F32, name="sf")
         for j in range(PACK):
             nc.scalar.activation(sf[:, j, :], sig_k[:, j, :], ACT.Copy, scale=fsc_k[:, j : j + 1])
+        vec_cols = ps.tile([P, P], F32, name="vec_cols", tag="bank0")
+        nc.tensor.transpose(vec_cols[:], vec_rows[:], ident[:])
+        rate_m = sb.tile([P, PACK], F32, name="rate_m")
+        nc.scalar.copy(rate_m[:], vec_cols[:, 0:PACK])
         neg_th = sb.tile([P, PACK], F32, name="neg_th")
-        nc.gpsimd.tensor_scalar(neg_th[:], th_m[:], -1.0, 0.0, ALU.mult, ALU.add)
+        nc.scalar.activation(neg_th[:], vec_cols[:, PACK : 2 * PACK], ACT.Copy, scale=-1.0)
 
         e_planes = sb.tile([P, PACK, Q], BF16, name="e_planes", align_bytes=64)
         for j in range(PACK):
@@ -137,9 +141,11 @@ def tile_attend_pursuitstep_kernel(tc, rows, code0, cs1, sig, fsc, atom_words, a
                 out=r[:], lhsT=w.bitcast(FP8X4), lhsT_scale=s,
                 rhs=cw_w[:].bitcast(FP8X4), rhs_scale=cw_s[:], start=True, stop=True,
             )
-            nc.vector.scalar_tensor_tensor(
-                e_planes[:, j, :], r[:], neg_fsc[:, j : j + 1], sf[:, j, :], ALU.mult, ALU.add
-            )
+            pieces = [slice(0, Q)] if j < PACK - 1 else [slice(HALF, Q), slice(0, HALF)]
+            for cols in pieces:
+                nc.vector.scalar_tensor_tensor(
+                    e_planes[:, j, cols], r[:, cols], neg_fsc[:, j : j + 1], sf[:, j, cols], ALU.mult, ALU.add
+                )
 
         e_w = sb.tile([P, Q], U32, name="e_w", align_bytes=64)
         e_s = sb.tile([P, Q], U8, name="e_s", align_bytes=64)
@@ -160,14 +166,21 @@ def tile_attend_pursuitstep_kernel(tc, rows, code0, cs1, sig, fsc, atom_words, a
             part = slice((j % 2) * P, (j % 2 + 1) * P)
             a = ps.tile([P, Q], F32, name=f"a{j}", tag=f"bank{j}")
             nc.tensor.matmul_mx(
-                out=a[:], lhsT=atom_w_g[j // 2][:, part].bitcast(FP8X4), lhsT_scale=atom_sc_g[j // 2][:, part],
+                out=a[:], lhsT=atom_w_g[j // 2][:, part].bitcast(FP8X4), lhsT_scale=atom_sc_g[j],
                 rhs=e_w[:].bitcast(FP8X4), rhs_scale=e_s[:], start=True, stop=True,
             )
             x = sb.tile([P, Q], F32, name=f"x{j}")
-            nc.vector.scalar_tensor_tensor(x[:], a[:], rate_m[:, j : j + 1], code_m[:, j, :], ALU.mult, ALU.add)
             y = sb.tile([P, Q], F32, name=f"y{j}")
             if j < PACK - 1:
+                nc.vector.scalar_tensor_tensor(x[:], a[:], rate_m[:, j : j + 1], code_m[:, j, :], ALU.mult, ALU.add)
                 nc.scalar.activation(y[:], x[:], ACT.Relu, bias=neg_th[:, j : j + 1])
+                nc.sync.dma_start(out[cols, :], y[:])
             else:
-                nc.vector.tensor_scalar(y[:], x[:], th_m[:, j : j + 1], 0.0, ALU.subtract, ALU.max)
-            nc.sync.dma_start(out[cols, :], y[:])
+                halves = [slice(0, HALF), slice(HALF, Q)]
+                for half in halves:
+                    nc.vector.scalar_tensor_tensor(
+                        x[:, half], a[:, half], rate_m[:, j : j + 1], code_m[:, j, half], ALU.mult, ALU.add
+                    )
+                for half in halves:
+                    nc.vector.tensor_scalar(y[:, half], x[:, half], neg_th[:, j : j + 1], 0.0, ALU.add, ALU.max)
+                nc.sync.dma_start(out[cols, :], y[:])

@@ -86,7 +86,8 @@ def tile_attend_pursuitstep_kernel(tc, rows, code0, cs1, sig, fsc, atom_words, a
             words = g[:].bitcast(F32)
             xt = ps.tile([P, 2, P], F32, name=f"xt{j}", tag=f"bank{j}")
             for u in range(2):
-                nc.tensor.transpose(xt[:, u, :], words[:, u : I // 2 : 2], ident[:])
+                picked = words[:, u : I // 2 : 2] if j == 0 else words[:, u * P : (u + 1) * P]
+                nc.tensor.transpose(xt[:, u, :], picked, ident[:])
             nc.scalar.copy(rt.bitcast(F32), xt[:].rearrange("s u p -> s p u"))
 
         plane0_bf = sb.tile([P, T], BF16, name="plane0_bf", align_bytes=64)
@@ -94,7 +95,8 @@ def tile_attend_pursuitstep_kernel(tc, rows, code0, cs1, sig, fsc, atom_words, a
         gs = [sb.tile([P, I], BF16, name=f"g{j}", align_bytes=64) for j in range(PACK)]
         nc.scalar.activation(gs[0][:], plane0_bf[:].indirect(offsets[:]), ACT.Copy)
         for j in range(1, PACK):
-            nc.vector.tensor_copy(gs[j][:], planes[j][:].indirect(offsets[:]))
+            dealt = gs[j][:].rearrange("p (u s e) -> p s u e", u=2, e=2)
+            nc.vector.tensor_copy(dealt, planes[j][:].indirect(offsets[:]))
         rt01 = sb.tile([P, 2 * P, PACK], BF16, name="rt01", align_bytes=64)
         rt2 = sb.tile([P, P, PACK], BF16, name="rt2", align_bytes=64)
         rt3 = sb.tile([P, P, PACK], BF16, name="rt3", align_bytes=64)

from contextlib import ExitStack

import concourse.mybir as mybir
from concourse.masks import make_identity

D, T, I, Q = 512, 1024, 512, 256
FLOPS = 2 * 2 * D * I * Q

F32 = mybir.dt.float32
BF16 = mybir.dt.bfloat16
I32 = mybir.dt.int32
U32 = mybir.dt.uint32
U16 = mybir.dt.uint16
U8 = mybir.dt.uint8
FP8X4 = mybir.dt.float8_e4m3fn_x4
ALU = mybir.AluOpType
ACT = mybir.ActivationFunctionType

P = 128
PACK = 4
HALF = Q // 2


def walk_planes(ap):
    return ap.rearrange("p t (c i) -> p c t i", i=4)


def walk_grouped(ap):
    return ap.rearrange("p (c i) t -> p c t i", i=4)


def tile_attend_pursuitstep_kernel(tc, rows, code0, cs1, sig, fsc, atom_words, atom_scales, rate, th, offs, out):
    nc = tc.nc
    with ExitStack() as ctx:
        sb = ctx.enter_context(tc.tile_pool(name="sb", bufs=1))
        last = ctx.enter_context(tc.tile_pool(name="last", bufs=1))
        ps = ctx.enter_context(tc.psum_pool(name="ps", bufs=1))

        offsets = sb.tile([P, I // 16], U16, name="offsets")
        nc.sync.dma_start(offsets[:], offs)
        cs_k = sb.tile([P, PACK], F32, name="cs_k")
        nc.sync.dma_start(cs_k[:], cs1.rearrange("(p t) o -> p (t o)", t=PACK))
        code_k = sb.tile([P, PACK, Q], F32, name="code_k")
        nc.sync.dma_start(code_k[:], code0.rearrange("(p t) q -> p t q", t=PACK))

        rows_k = rows.rearrange("(p t) c -> t p c", t=PACK)
        planes = [sb.tile([P, T], F32, name=f"plane{j}", align_bytes=64) for j in range(PACK - 1)]
        planes.append(last.tile([P, T], F32, name="plane3", align_bytes=64, offset=0))
        nc.sync.dma_start(planes[0][:], rows_k[0])
        atom_sc = sb.tile([P, T], U8, name="atom_sc", align_bytes=64)
        nc.vector.memset(atom_sc[:].bitcast(I32), 0)
        for r in range(4):
            nc.sync.dma_start(atom_sc[r:P:32, :].bitcast(I32), atom_scales[0, r:16:4, :].bitcast(I32))
        for j in range(1, PACK):
            nc.sync.dma_start(planes[j][:], rows_k[j])
        atom_w = sb.tile([P, T], I32, name="atom_w", align_bytes=64)
        nc.sync.dma_start(atom_w[:], atom_words[0].rearrange("p n t -> p (n t)").bitcast(I32))
        fsc_k = sb.tile([P, PACK], F32, name="fsc_k")
        nc.sync.dma_start(fsc_k[:], fsc.rearrange("(p t) o -> p (t o)", t=PACK))
        sig_k = sb.tile([P, PACK, Q], F32, name="sig_k")
        nc.sync.dma_start(sig_k[:], sig.rearrange("(p t) q -> p t q", t=PACK))
        vec_rows = sb.tile([P, P], F32, name="vec_rows")
        nc.gpsimd.memset(vec_rows[:], 0.0)
        nc.sync.dma_start(vec_rows[0:PACK, :], rate.rearrange("(j m) o -> j (m o)", m=P))
        nc.sync.dma_start(vec_rows[PACK : 2 * PACK, :], th.rearrange("(j m) o -> j (m o)", m=P))
        code_m = sb.tile([P, PACK, Q], F32, name="code_m")
        nc.sync.dma_start(code_m[:], code0.rearrange("(j m) q -> m j q", m=P))

        ident = sb.tile([P, P], F32, name="ident")
        make_identity(nc, ident[:])

        cw = sb.tile([P, Q, PACK], BF16, name="cw", align_bytes=64)
        nc.vector.tensor_tensor(
            walk_grouped(cw[:]),
            walk_planes(code_k[:]),
            cs_k[:].unsqueeze(1).unsqueeze(3).to_broadcast([P, Q // 4, PACK, 4]),
            ALU.mult,
        )
        cw_w = sb.tile([P, Q], U32, name="cw_w", align_bytes=64)
        cw_s = sb.tile([P, Q], U8, name="cw_s", align_bytes=64)
        nc.vector.quantize_mx(out=cw_w[:].bitcast(FP8X4), scales=cw_s[:], in_=cw[:].rearrange("p q t -> p (q t)"))
        sc_early = sb.tile([P, 3 * P], U8, name="sc_early", align_bytes=64)
        nc.vector.tensor_copy(sc_early[:], atom_sc[:].indirect(offsets[:, :24]))

        def turn(j, g, rt):
            words = g[:].bitcast(F32)
            xt = ps.tile([P, 2, P], F32, name=f"xt{j}", tag=f"bank{j}")
            for u in range(2):
                picked = words[:, u : I // 2 : 2] if j == 0 else words[:, u * P : (u + 1) * P]
                nc.tensor.transpose(xt[:, u, :], picked, ident[:])
            nc.scalar.copy(rt.bitcast(F32), xt[:].rearrange("s u p -> s p u"))

        plane0_bf = sb.tile([P, T], BF16, name="plane0_bf", align_bytes=64)
        nc.scalar.activation(plane0_bf[:], planes[0][:], ACT.Copy)
        gs = [sb.tile([P, I], BF16, name=f"g{j}", align_bytes=64) for j in range(PACK)]
        nc.scalar.activation(gs[0][:], plane0_bf[:].indirect(offsets[:]), ACT.Copy)
        for j in range(1, PACK):
            dealt = gs[j][:].rearrange("p (u s e) -> p s u e", u=2, e=2)
            nc.vector.tensor_copy(dealt, planes[j][:].indirect(offsets[:]))
        rt01 = sb.tile([P, 2 * P, PACK], BF16, name="rt01", align_bytes=64)
        rt2 = sb.tile([P, P, PACK], BF16, name="rt2", align_bytes=64)
        rt3 = sb.tile([P, P, PACK], BF16, name="rt3", align_bytes=64)
        turn(0, gs[0], rt01[:, :P, :])
        turn(1, gs[1], rt01[:, P:, :])
        turn(2, gs[2], rt2[:])
        turn(3, gs[3], rt3[:])

        def quantise(w, name, rt):
            s = sb.tile([P, w.shape[1]], U8, name=f"rt_s{name}", align_bytes=64)
            nc.vector.quantize_mx(out=w[:].bitcast(FP8X4), scales=s[:], in_=rt[:].rearrange("s p t -> s (p t)"))
            return s

        w01 = last.tile([P, 2 * P], U32, name="rt_w01", align_bytes=64, offset=0)
        s01 = quantise(w01, "01", rt01)
        sc_late = last.tile([P, P], U8, name="sc_late", align_bytes=64, offset=1024)
        nc.vector.tensor_copy(sc_late[:], atom_sc[:].indirect(offsets[:, 24:]))
        atom_sc_g = [sc_early[:, j * P : (j + 1) * P] for j in range(PACK - 1)] + [sc_late[:]]
        w2 = sb.tile([P, P], U32, name="rt_w2", align_bytes=64)
        s2 = quantise(w2, "2", rt2)
        atom_w_g = [sb.tile([P, I // 2], U32, name="atom_w_g0", align_bytes=64)]
        nc.vector.tensor_copy(atom_w_g[0][:], atom_w[:].bitcast(U32).indirect(offsets[:, :16]))
        w3 = sb.tile([P, P], U32, name="rt_w3", align_bytes=64)
        s3 = quantise(w3, "3", rt3)
        rtq = [(w01[:, :P], s01[:, :P]), (w01[:, P:], s01[:, P:]), (w2[:], s2[:]), (w3[:], s3[:])]

        neg_fsc = sb.tile([P, PACK], F32, name="neg_fsc")
        nc.gpsimd.tensor_scalar(neg_fsc[:], fsc_k[:], -1.0, 0.0, ALU.mult, ALU.add)
        sf = sb.tile([P, PACK, Q], F32, name="sf")
        for j in range(PACK):
            nc.scalar.activation(sf[:, j, :], sig_k[:, j, :], ACT.Copy, scale=fsc_k[:, j : j + 1])
        vec_cols = ps.tile([P, P], F32, name="vec_cols", tag="bank0")
        nc.tensor.transpose(vec_cols[:], vec_rows[:], ident[:])
        rate_m = sb.tile([P, PACK], F32, name="rate_m")
        nc.scalar.copy(rate_m[:], vec_cols[:, 0:PACK])
        neg_th = sb.tile([P, PACK], F32, name="neg_th")
        nc.scalar.activation(neg_th[:], vec_cols[:, PACK : 2 * PACK], ACT.Copy, scale=-1.0)

        e_planes = sb.tile([P, PACK, Q], BF16, name="e_planes", align_bytes=64)
        for j in range(PACK):
            w, s = rtq[j]
            r = ps.tile([P, Q], F32, name=f"r{j}", tag=f"bank{4 + j}")
            nc.tensor.matmul_mx(
                out=r[:], lhsT=w.bitcast(FP8X4), lhsT_scale=s,
                rhs=cw_w[:].bitcast(FP8X4), rhs_scale=cw_s[:], start=True, stop=True,
            )
            pieces = [slice(0, Q)] if j < PACK - 1 else [slice(HALF, Q), slice(0, HALF)]
            for cols in pieces:
                nc.vector.scalar_tensor_tensor(
                    e_planes[:, j, cols], r[:, cols], neg_fsc[:, j : j + 1], sf[:, j, cols], ALU.mult, ALU.add
                )

        e_w = sb.tile([P, Q], U32, name="e_w", align_bytes=64)
        e_s = sb.tile([P, Q], U8, name="e_s", align_bytes=64)
        es = [sb.tile([P, HALF, PACK], BF16, name=f"e{h}", tag=f"e{h}", align_bytes=64) for h in range(2)]
        nc.vector.tensor_copy(walk_grouped(es[0][:]), walk_planes(e_planes[:, :, :HALF]))
        nc.scalar.copy(walk_grouped(es[1][:]), walk_planes(e_planes[:, :, HALF:]))
        for h in range(2):
            cols = slice(h * HALF, (h + 1) * HALF)
            nc.vector.quantize_mx(
                out=e_w[:, cols].bitcast(FP8X4), scales=e_s[:, cols], in_=es[h][:].rearrange("p q t -> p (q t)")
            )

        atom_w_g.append(sb.tile([P, I // 2], U32, name="atom_w_g1", tag="e1", align_bytes=64))
        nc.vector.tensor_copy(atom_w_g[1][:], atom_w[:].bitcast(U32).indirect(offsets[:, 16:]))

        for j in range(PACK):
            cols = slice(j * P, (j + 1) * P)
            part = slice((j % 2) * P, (j % 2 + 1) * P)
            a = ps.tile([P, Q], F32, name=f"a{j}", tag=f"bank{j}")
            nc.tensor.matmul_mx(
                out=a[:], lhsT=atom_w_g[j // 2][:, part].bitcast(FP8X4), lhsT_scale=atom_sc_g[j],
                rhs=e_w[:].bitcast(FP8X4), rhs_scale=e_s[:], start=True, stop=True,
            )
            x = sb.tile([P, Q], F32, name=f"x{j}")
            y = sb.tile([P, Q], F32, name=f"y{j}")
            if j < PACK - 1:
                nc.vector.scalar_tensor_tensor(x[:], a[:], rate_m[:, j : j + 1], code_m[:, j, :], ALU.mult, ALU.add)
                nc.scalar.activation(y[:], x[:], ACT.Relu, bias=neg_th[:, j : j + 1])
                nc.sync.dma_start(out[cols, :], y[:])
            else:
                halves = [slice(0, HALF), slice(HALF, Q)]
                for half in halves:
                    nc.vector.scalar_tensor_tensor(
                        x[:, half], a[:, half], rate_m[:, j : j + 1], code_m[:, j, half], ALU.mult, ALU.add
                    )
                for half in halves:
                    nc.vector.tensor_scalar(y[:, half], x[:, half], neg_th[:, j : j + 1], 0.0, ALU.add, ALU.max)
                nc.sync.dma_start(out[cols, :], y[:])
